import numpy as np
import ml_dtypes


def mxq(x, axis, fmt="e4m3"):
    dtype, down = {"e4m3": (ml_dtypes.float8_e4m3fn, 7), "e5m2": (ml_dtypes.float8_e5m2, 14)}[fmt]
    v = np.moveaxis(np.asarray(x, np.float32).astype(ml_dtypes.bfloat16).astype(np.float64), axis, -1)
    blocks = v.reshape(v.shape[:-1] + (-1, 32))
    amax = np.abs(blocks).max(-1, keepdims=True)
    byte = np.maximum(np.where(amax > 0, np.frexp(amax)[1] - 1 + 127, 0) - down, 1)
    scale = np.exp2(byte - 127.0)
    codes = (blocks / scale).astype(np.float32).astype(dtype).astype(np.float64)
    return np.moveaxis((codes * scale).reshape(v.shape), -1, axis)


WIDE = False


def mx_kscale(k):
    if not WIDE:
        return np.ones(k)
    levels = np.array([30, -30])
    if k % 512:
        return np.exp2(np.random.permutation(np.resize(levels, k // 32))).repeat(32)
    a = np.empty((k // 512, 16))
    for p in range(k // 512):
        a[p, :8] = np.random.permutation(np.resize(levels, 8))
        for g in range(8):
            far = levels[np.abs(levels - a[p, g]) >= 10]
            a[p, g + 8] = far[np.random.randint(len(far))]
    return np.exp2(a.ravel()).repeat(32)


def f64(x):
    return np.asarray(x).astype(np.float64)


def striped(idx):
    return np.tile(np.asarray(idx).reshape(-1, 16).T, (8, 1)).astype(np.uint16)


def unstriped(offs):
    return offs[:16].T.reshape(-1).astype(np.int64)


E2M1 = np.array([0.0, 0.5, 1.0, 1.5, 2.0, 3.0, 4.0, 6.0, -0.0, -0.5, -1.0, -1.5, -2.0, -3.0, -4.0, -6.0])


def pack_weight(w, fmt):
    k, n = w.shape
    w = f64(np.asarray(w, np.float32).astype(ml_dtypes.bfloat16)).reshape(k // 32, 32, n)
    amax = np.abs(w).max(1)
    if fmt in ("e4m3", "e5m2"):
        byte = np.frexp(amax)[1] - 1 + 127 - (7 if fmt == "e4m3" else 14)
    else:
        mant, ex = np.frexp(amax / 6.0)
        byte = np.where(mant > 0.5, ex, ex - 1) + 127
    byte = np.clip(np.where(amax > 0, byte, 1), 1, 254)
    scaled = (w * np.exp2(127.0 - byte)[:, None, :]).reshape(k, n).astype(np.float32)
    by_word = np.ascontiguousarray(scaled.reshape(k // 512, 128, 4, n).transpose(0, 1, 3, 2))
    if fmt in ("e4m3", "e5m2"):
        words = by_word.astype(ml_dtypes.float8_e4m3fn if fmt == "e4m3" else ml_dtypes.float8_e5m2).view(np.uint8)
    else:
        c = by_word.astype(ml_dtypes.float4_e2m1fn).view(np.uint8) & 0xF
        words = (c[..., 0::2] | (c[..., 1::2] << 4)).reshape(k // 512, 128, 2 * n)
    return np.ascontiguousarray(words), np.ascontiguousarray(byte.astype(np.uint8).reshape(k // 512, 16, n))


def unpack_weight(words, scales, fmt):
    g, _, n = scales.shape
    words = np.ascontiguousarray(words).reshape(g, 128, n, -1)
    if fmt in ("e4m3", "e5m2"):
        vals = words.view(ml_dtypes.float8_e4m3fn if fmt == "e4m3" else ml_dtypes.float8_e5m2).astype(np.float64)
    else:
        nib = np.empty((g, 128, n, 4), np.uint8)
        nib[..., 0::2] = words & 0xF
        nib[..., 1::2] = words >> 4
        vals = E2M1[nib]
    vals = vals * np.repeat(np.exp2(scales.astype(np.float64) - 127.0), 8, axis=1)[..., None]
    return vals.transpose(0, 1, 3, 2).reshape(g * 512, n)


K, T, J, R, M, Q, O, U, X, D, N, E = 512, 1024, 256, 512, 512, 128, 64, 64, 128, 256, 256, 512


def setup_inputs():
    n = np.random.standard_normal
    idx = np.random.permutation(T)[:J]
    idx2 = np.random.permutation(J)[:O]
    idx3 = np.random.permutation(J)[:U]
    idx4 = np.random.permutation(E)[:D]
    idx5 = np.random.permutation(E)[:D]
    fk = mx_kscale(K)
    fm = mx_kscale(M)
    fr = mx_kscale(R)
    xtp = pack_weight(n((K, T)) / fk[:, None], "e2m1")
    wp = pack_weight(n((K, R)) * 1 / np.sqrt(K) * fk[:, None], "e4m3")
    xcp = pack_weight(n((M, Q)) / fm[:, None], "e4m3")
    wgp = pack_weight(n((M, R)) * 1 / np.sqrt(M) * fm[:, None] * fr, "e5m2")
    wbp = pack_weight(n((R, N)) * 1 / np.sqrt(R) / fr[:, None], "e2m1")
    return {
        "xt_words": xtp[0],
        "xt_scales": xtp[1],
        "w_words": wp[0],
        "w_scales": wp[1],
        "xc_words": xcp[0],
        "xc_scales": xcp[1],
        "wg_words": wgp[0],
        "wg_scales": wgp[1],
        "wb_words": wbp[0],
        "wb_scales": wbp[1],
        "offs": striped(idx),
        "offs2": striped(idx2),
        "offs3": striped(idx3),
        "offs4": striped(idx4),
        "offs5": striped(idx5),
    }


def reference(xt_words, xt_scales, w_words, w_scales, xc_words, xc_scales, wg_words, wg_scales, wb_words, wb_scales, offs, offs2, offs3, offs4, offs5):
    idx = unstriped(offs)
    idx2 = unstriped(offs2)
    idx3 = unstriped(offs3)
    idx4 = unstriped(offs4)
    idx5 = unstriped(offs5)
    xtu = unpack_weight(xt_words, xt_scales, "e2m1")
    wu = unpack_weight(w_words, w_scales, "e4m3")
    xcu = unpack_weight(xc_words, xc_scales, "e4m3")
    wgu = unpack_weight(wg_words, wg_scales, "e5m2")
    wbu = unpack_weight(wb_words, wb_scales, "e2m1")
    xtidxg = xtu[:, idx]
    a = wu.T @ xtidxg
    g0 = wgu.T @ xcu
    ga = g0[:, 0:1]
    gb = g0[:, 64:65]
    h1 = a[:, idx2] * ga
    h2 = a[:, idx3] * gb
    h3 = np.concatenate([h1, h2], axis=1)
    hid = np.concatenate([h3, g0], axis=1)
    hidq = mxq(hid, 0, "e5m2")
    p = wbu.T @ hidq
    pa = np.zeros((N, E))
    pa[:, idx4] = p
    pb = np.zeros((N, E))
    pb[:, idx5] = p
    y = pa + pb
    return y

@@ -1,0 +1,184 @@
+from contextlib import ExitStack
+
+import concourse.mybir as mybir
+
+K, T, J, R, M, Q, O, U, X, D, N, E = 512, 1024, 256, 512, 512, 128, 64, 64, 128, 256, 256, 512
+FLOPS = 2 * K * R * J + 2 * M * R * Q + 2 * R * N * D
+
+F32 = mybir.dt.float32
+BF16 = mybir.dt.bfloat16
+I32 = mybir.dt.int32
+U32 = mybir.dt.uint32
+U16 = mybir.dt.uint16
+U8 = mybir.dt.uint8
+E4M3X4 = mybir.dt.float8_e4m3fn_x4
+E5M2X4 = mybir.dt.float8_e5m2_x4
+E2M1X4 = mybir.dt.float4_e2m1fn_x4
+COPY = mybir.ActivationFunctionType.Copy
+ADD = mybir.AluOpType.add
+
+P = 128
+PACK = 4
+QUADS = 4
+
+
+def tile_list_ctxthirds_solo_one_pagetwice_kernel(
+    tc, xt_words, xt_scales, w_words, w_scales, xc_words, xc_scales, wg_words, wg_scales,
+    wb_words, wb_scales, offs, offs2, offs3, offs4, offs5, out,
+):
+    nc = tc.nc
+    with ExitStack() as ctx:
+        sb = ctx.enter_context(tc.tile_pool(name="sb", bufs=1))
+        ps = ctx.enter_context(tc.psum_pool(name="ps", bufs=1))
+
+        def tile(name, shape, dtype, tag=""):
+            return sb.tile(shape, dtype, name=name, tag=tag, align_bytes=64)
+
+        def by_quadrant(scales):
+            return scales[0].bitcast(I32).rearrange("(q r) n -> r q n", r=4)
+
+        def load_list(name, src):
+            lst = sb.tile(list(src.shape), U16, name=name)
+            nc.sync.dma_start(lst[:], src)
+            return lst
+
+        def load_words(name, src, cols):
+            words = tile(name, [P, cols], U32, tag=name)
+            nc.sync.dma_start(words[:].bitcast(I32), src[0].rearrange("p n t -> p (n t)").bitcast(I32))
+            return words
+
+        def spread(plane, rows):
+            for q in range(QUADS):
+                nc.vector.tensor_copy(plane[32 * q : 32 * q + 4, :].bitcast(I32), rows[:, q, :])
+
+        planes = tile("planes", [P, 2 * R + Q], U8)
+        xt_plane = tile("xt_plane", [P, T], U8)
+        wb_rows = tile("wb_rows", [P, 2, N // 4], I32)
+        nc.vector.memset(wb_rows[0:64, :, :], 0)
+        for plane in (planes, xt_plane):
+            nc.vector.memset(plane[:].bitcast(I32), 0)
+        pages = [[tile("page%d%d" % (h, k), [P, E], F32) for k in range(2)] for h in range(2)]
+
+        for h in range(2):
+            nc.vector.memset(pages[h][0][:], 0.0)
+            nc.gpsimd.memset(pages[h][1][:], 0.0)
+
+        rows = tile("rows", [4, QUADS, (2 * R + Q) // 4], I32)
+        xt_rows = tile("xt_rows", [4, QUADS, T // 4], I32)
+        nc.scalar.dma_start(rows[:, :, 0 : R // 4], by_quadrant(wg_scales))
+        nc.sync.dma_start(rows[:, :, R // 4 : R // 2], by_quadrant(w_scales))
+        nc.scalar.dma_start(rows[:, :, R // 2 :], by_quadrant(xc_scales))
+        nc.sync.dma_start(xt_rows[:], by_quadrant(xt_scales))
+        wg_raw = load_words("wg_raw", wg_words, R)
+        idx = load_list("idx", offs)
+        xc_w = load_words("xc_w", xc_words, Q)
+        xt_w = tile("xt_w", [P, T], U16)
+        nc.sync.dma_start(xt_w[:].bitcast(I32), xt_words[0].bitcast(I32))
+        w_raw = load_words("w_raw", w_words, R)
+        idx2 = load_list("idx2", offs2)
+        idx3 = load_list("idx3", offs3)
+        wb_w = tile("wb_w", [P, 2 * N], U8)
+        nc.sync.dma_start(wb_w[:].bitcast(I32), wb_words[0].bitcast(I32))
+        page_lists = [load_list("idx4", offs4), load_list("idx5", offs5)]
+        wb_src = wb_scales[0].bitcast(I32).rearrange("(half q r) n -> q r half n", half=2, r=4)
+        for q in range(2):
+            nc.sync.dma_start(wb_rows[32 * q : 32 * q + 4, :, :], wb_src[q])
+
+        def deal_words(name, src):
+            dealt = tile(name, [P, PACK, P], U32)
+            nc.scalar.copy(dealt[:].rearrange("p t m -> p m t"), src.rearrange("p (m t) -> p m t", t=PACK))
+            return dealt
+
+        def deal_bytes(name, src, engine):
+            dealt = tile(name, [P, PACK, P], U8)
+            engine.tensor_copy(dealt[:], src.rearrange("p (m t) -> p t m", t=PACK))
+            return dealt
+
+        spread(planes, rows)
+        wg_s = deal_bytes("wg_s", planes[:, 0:R], nc.vector)
+        wg_w = deal_words("wg_w", wg_raw[:])
+        g_ps = ps.tile([P, PACK, Q], F32, name="g_ps")
+        for t in range(PACK):
+            nc.tensor.matmul_mx(
+                out=g_ps[:, t, :], lhsT=wg_w[:, t, :].bitcast(E5M2X4), lhsT_scale=wg_s[:, t, :],
+                rhs=xc_w[:].bitcast(E4M3X4), rhs_scale=planes[:, 2 * R :], start=True, stop=True,
+            )
+
+        spread(xt_plane, xt_rows)
+        xg_s = tile("xg_s", [P, J], U8)
+        nc.vector.tensor_copy(xg_s[:], xt_plane[:].indirect(idx[:]))
+        w_w = deal_words("w_w", w_raw[:])
+        w_s = deal_bytes("w_s", planes[:, R : 2 * R], nc.vector)
+        xg_w = tile("xg_w", [P, J], U16)
+        nc.vector.tensor_copy(xg_w[:], xt_w[:].indirect(idx[:]))
+
+        gains = tile("gains", [P, PACK, 2], F32)
+        nc.scalar.copy(gains[:], g_ps[:, :, 0 : Q : O])
+        g_bf = tile("g_bf", [P, Q, PACK], BF16, tag="w_raw")
+        nc.scalar.copy(g_bf[:], g_ps[:].rearrange("p t q -> p q t"))
+
+        a_ps = [ps.tile([P, J], F32, name="a_ps%d" % t) for t in range(PACK)]
+        for t in range(PACK):
+            nc.tensor.matmul_mx(
+                out=a_ps[t][:], lhsT=w_w[:, t, :].bitcast(E4M3X4), lhsT_scale=w_s[:, t, :],
+                rhs=xg_w[:].bitcast(E2M1X4), rhs_scale=xg_s[:], start=True, stop=True,
+            )
+        nc.vector.tensor_copy(wb_rows[64:P, 0, :], wb_rows[0:64, 1, :])
+        wb_plane = wb_rows[:, 0, :].bitcast(U8)
+
+        def quantise(name, values):
+            codes = tile(name + "_codes", [P, P], U32)
+            plane = tile(name + "_plane", [P, P], U8)
+            nc.vector.quantize_mx(out=codes[:].bitcast(E5M2X4), scales=plane[:], in_=values[:].rearrange("p d t -> p (d t)"))
+            return codes, plane
+
+        def project(bank, h, codes, plane):
+            nc.tensor.matmul_mx(
+                out=bank, lhsT=wb_w[:, 2 * P * h : 2 * P * (h + 1)].bitcast(E2M1X4), lhsT_scale=wb_plane[:, P * h : P * (h + 1)],
+                rhs=codes[:].bitcast(E5M2X4), rhs_scale=plane[:], start=True, stop=True,
+            )
+
+        def put(engine, h, k, src, base, d0, d1):
+            window = pages[h][k][:].indirect(page_lists[k][:, d0 // 16 : d1 // 16])
+            if engine == "vector":
+                nc.vector.tensor_copy(window, src[:, d0 - base : d1 - base])
+            else:
+                nc.scalar.activation(window, src[:, d0 - base : d1 - base], COPY)
+
+        g_codes, g_plane = quantise("g", g_bf)
+
+        h32 = tile("h32", [P, PACK, X], F32)
+        for t in range(PACK):
+            a_t = tile("a%d" % t, [P, J], F32)
+            nc.vector.tensor_copy(a_t[:], a_ps[t][:])
+            nc.scalar.activation(h32[:, t, 0:O], a_t[:].indirect(idx2[:]), COPY, scale=gains[:, t, 0:1])
+            nc.scalar.activation(h32[:, t, O:X], a_t[:].indirect(idx3[:]), COPY, scale=gains[:, t, 1:2])
+
+        pg_ps = ps.tile([P, 2, Q], F32, name="pg_ps")
+        for h in range(2):
+            project(pg_ps[:, h, :], h, g_codes, g_plane)
+        pg = tile("pg", [P, 2, Q], F32)
+        nc.vector.tensor_copy(pg[:], pg_ps[:])
+
+        h_bf = tile("h_bf", [P, X, PACK], BF16)
+        nc.vector.tensor_copy(h_bf[:].rearrange("p (c i) t -> p c t i", i=4), h32[:].rearrange("p t (c i) -> p c t i", i=4))
+        h_codes, h_plane = quantise("h", h_bf)
+        ph_ps = ps.tile([P, 2, X], F32, name="ph_ps")
+        for h in range(2):
+            project(ph_ps[:, h, :], h, h_codes, h_plane)
+        put("vector", 0, 0, pg[:, 0, :], X, X, D)
+        put("scalar", 0, 1, pg[:, 0, :], X, X, D)
+        put("scalar", 1, 1, pg[:, 1, :], X, X, D)
+        put("scalar", 1, 0, pg[:, 1, :], X, X, D)
+        ph = tile("ph", [P, 2, X], F32)
+        nc.vector.tensor_copy(ph[:], ph_ps[:])
+        sums = [tile("sum%d" % h, [P, E], F32) for h in range(2)]
+        for h in range(2):
+            put("vector", h, 0, ph[:, h, :], 0, 0, X)
+            put("scalar", h, 1, ph[:, h, :], 0, 0, X)
+        nc.vector.tensor_tensor(sums[0][:], pages[0][0][:], pages[0][1][:], ADD)
+        nc.sync.dma_start(out[0:P, :], sums[0][:])
+        for c in range(2):
+            cols = slice(c * E // 2, (c + 1) * E // 2)
+            nc.vector.tensor_tensor(sums[1][:, cols], pages[1][0][:, cols], pages[1][1][:, cols], ADD)
+            nc.sync.dma_start(out[P:N, cols], sums[1][:, cols])

@@ -53,9 +53,8 @@ def tile_list_ctxthirds_solo_one_pagetwice_kernel(
 
         planes = tile("planes", [P, 2 * R + Q], U8)
         xt_plane = tile("xt_plane", [P, T], U8)
-        wb_rows = tile("wb_rows", [P, 2, N // 4], I32)
-        nc.vector.memset(wb_rows[0:64, :, :], 0)
-        for plane in (planes, xt_plane):
+        wb_plane = tile("wb_plane", [P, N], U8)
+        for plane in (planes, xt_plane, wb_plane):
             nc.vector.memset(plane[:].bitcast(I32), 0)
         pages = [[tile("page%d%d" % (h, k), [P, E], F32) for k in range(2)] for h in range(2)]
 
@@ -74,15 +73,14 @@ def tile_list_ctxthirds_solo_one_pagetwice_kernel(
         xc_w = load_words("xc_w", xc_words, Q)
         xt_w = tile("xt_w", [P, T], U16)
         nc.sync.dma_start(xt_w[:].bitcast(I32), xt_words[0].bitcast(I32))
-        w_raw = load_words("w_raw", w_words, R)
         idx2 = load_list("idx2", offs2)
         idx3 = load_list("idx3", offs3)
+        w_raw = load_words("w_raw", w_words, R)
+        wb_rows = tile("wb_rows", [4, QUADS, N // 4], I32)
+        nc.sync.dma_start(wb_rows[:], by_quadrant(wb_scales))
         wb_w = tile("wb_w", [P, 2 * N], U8)
         nc.sync.dma_start(wb_w[:].bitcast(I32), wb_words[0].bitcast(I32))
         page_lists = [load_list("idx4", offs4), load_list("idx5", offs5)]
-        wb_src = wb_scales[0].bitcast(I32).rearrange("(half q r) n -> q r half n", half=2, r=4)
-        for q in range(2):
-            nc.sync.dma_start(wb_rows[32 * q : 32 * q + 4, :, :], wb_src[q])
 
         def deal_words(name, src):
             dealt = tile(name, [P, PACK, P], U32)
@@ -123,8 +121,7 @@ def tile_list_ctxthirds_solo_one_pagetwice_kernel(
                 out=a_ps[t][:], lhsT=w_w[:, t, :].bitcast(E4M3X4), lhsT_scale=w_s[:, t, :],
                 rhs=xg_w[:].bitcast(E2M1X4), rhs_scale=xg_s[:], start=True, stop=True,
             )
-        nc.vector.tensor_copy(wb_rows[64:P, 0, :], wb_rows[0:64, 1, :])
-        wb_plane = wb_rows[:, 0, :].bitcast(U8)
+        spread(wb_plane, wb_rows)
 
         def quantise(name, values):
             codes = tile(name + "_codes", [P, P], U32)
@@ -163,15 +160,16 @@ def tile_list_ctxthirds_solo_one_pagetwice_kernel(
         h_bf = tile("h_bf", [P, X, PACK], BF16)
         nc.vector.tensor_copy(h_bf[:].rearrange("p (c i) t -> p c t i", i=4), h32[:].rearrange("p t (c i) -> p c t i", i=4))
         h_codes, h_plane = quantise("h", h_bf)
-        ph_ps = ps.tile([P, 2, X], F32, name="ph_ps")
+        ph_ps = [ps.tile([P, X], F32, name="ph_ps%d" % h) for h in range(2)]
         for h in range(2):
-            project(ph_ps[:, h, :], h, h_codes, h_plane)
+            project(ph_ps[h][:], h, h_codes, h_plane)
         put("vector", 0, 0, pg[:, 0, :], X, X, D)
         put("scalar", 0, 1, pg[:, 0, :], X, X, D)
         put("scalar", 1, 1, pg[:, 1, :], X, X, D)
         put("scalar", 1, 0, pg[:, 1, :], X, X, D)
         ph = tile("ph", [P, 2, X], F32)
-        nc.vector.tensor_copy(ph[:], ph_ps[:])
+        nc.vector.tensor_copy(ph[:, 0, :], ph_ps[0][:])
+        nc.scalar.copy(ph[:, 1, :], ph_ps[1][:])
         sums = [tile("sum%d" % h, [P, E], F32) for h in range(2)]
         for h in range(2):
             put("vector", h, 0, ph[:, h, :], 0, 0, X)

@@ -60,7 +60,7 @@ def tile_list_ctxthirds_solo_one_pagetwice_kernel(
 
         for h in range(2):
             nc.vector.memset(pages[h][0][:], 0.0)
-            nc.gpsimd.memset(pages[h][1][:], 0.0)
+            nc.vector.memset(pages[h][1][:], 0.0)
 
         rows = tile("rows", [4, QUADS, (2 * R + Q) // 4], I32)
         xt_rows = tile("xt_rows", [4, QUADS, T // 4], I32)
@@ -84,7 +84,7 @@ def tile_list_ctxthirds_solo_one_pagetwice_kernel(
 
         def deal_words(name, src):
             dealt = tile(name, [P, PACK, P], U32)
-            nc.scalar.copy(dealt[:].rearrange("p t m -> p m t"), src.rearrange("p (m t) -> p m t", t=PACK))
+            nc.scalar.copy(dealt[:].rearrange("p t (c i) -> p c t i", i=4), src.rearrange("p (c i t) -> p c t i", i=4, t=PACK))
             return dealt
 
         def deal_bytes(name, src, engine):

@@ -67,9 +67,9 @@ def tile_list_ctxthirds_solo_one_pagetwice_kernel(
         nc.scalar.dma_start(rows[:, :, 0 : R // 4], by_quadrant(wg_scales))
         nc.sync.dma_start(rows[:, :, R // 4 : R // 2], by_quadrant(w_scales))
         nc.scalar.dma_start(rows[:, :, R // 2 :], by_quadrant(xc_scales))
+        idx = load_list("idx", offs)
         nc.sync.dma_start(xt_rows[:], by_quadrant(xt_scales))
         wg_raw = load_words("wg_raw", wg_words, R)
-        idx = load_list("idx", offs)
         xc_w = load_words("xc_w", xc_words, Q)
         xt_w = tile("xt_w", [P, T], U16)
         nc.sync.dma_start(xt_w[:].bitcast(I32), xt_words[0].bitcast(I32))

from contextlib import ExitStack

import concourse.mybir as mybir

K, T, J, R, M, Q, O, U, X, D, N, E = 512, 1024, 256, 512, 512, 128, 64, 64, 128, 256, 256, 512
FLOPS = 2 * K * R * J + 2 * M * R * Q + 2 * R * N * D

F32 = mybir.dt.float32
BF16 = mybir.dt.bfloat16
I32 = mybir.dt.int32
U32 = mybir.dt.uint32
U16 = mybir.dt.uint16
U8 = mybir.dt.uint8
E4M3X4 = mybir.dt.float8_e4m3fn_x4
E5M2X4 = mybir.dt.float8_e5m2_x4
E2M1X4 = mybir.dt.float4_e2m1fn_x4
COPY = mybir.ActivationFunctionType.Copy
ADD = mybir.AluOpType.add

P = 128
PACK = 4
QUADS = 4


def tile_list_ctxthirds_solo_one_pagetwice_kernel(
    tc, xt_words, xt_scales, w_words, w_scales, xc_words, xc_scales, wg_words, wg_scales,
    wb_words, wb_scales, offs, offs2, offs3, offs4, offs5, out,
):
    nc = tc.nc
    with ExitStack() as ctx:
        sb = ctx.enter_context(tc.tile_pool(name="sb", bufs=1))
        ps = ctx.enter_context(tc.psum_pool(name="ps", bufs=1))

        def tile(name, shape, dtype, tag=""):
            return sb.tile(shape, dtype, name=name, tag=tag, align_bytes=64)

        def by_quadrant(scales):
            return scales[0].bitcast(I32).rearrange("(q r) n -> r q n", r=4)

        def load_list(name, src):
            lst = sb.tile(list(src.shape), U16, name=name)
            nc.sync.dma_start(lst[:], src)
            return lst

        def load_words(name, src, cols):
            words = tile(name, [P, cols], U32, tag=name)
            nc.sync.dma_start(words[:].bitcast(I32), src[0].rearrange("p n t -> p (n t)").bitcast(I32))
            return words

        def spread(plane, rows):
            for q in range(QUADS):
                nc.vector.tensor_copy(plane[32 * q : 32 * q + 4, :].bitcast(I32), rows[:, q, :])

        planes = tile("planes", [P, 2 * R + Q], U8)
        xt_plane = tile("xt_plane", [P, T], U8)
        wb_plane = tile("wb_plane", [P, N], U8)
        for plane in (planes, xt_plane, wb_plane):
            nc.vector.memset(plane[:].bitcast(I32), 0)
        pages = [[tile("page%d%d" % (h, k), [P, E], F32) for k in range(2)] for h in range(2)]

        for h in range(2):
            nc.vector.memset(pages[h][0][:], 0.0)
            nc.vector.memset(pages[h][1][:], 0.0)

        rows = tile("rows", [4, QUADS, (2 * R + Q) // 4], I32)
        xt_rows = tile("xt_rows", [4, QUADS, T // 4], I32)
        nc.scalar.dma_start(rows[:, :, 0 : R // 4], by_quadrant(wg_scales))
        nc.sync.dma_start(rows[:, :, R // 4 : R // 2], by_quadrant(w_scales))
        nc.scalar.dma_start(rows[:, :, R // 2 :], by_quadrant(xc_scales))
        idx = load_list("idx", offs)
        nc.sync.dma_start(xt_rows[:], by_quadrant(xt_scales))
        wg_raw = load_words("wg_raw", wg_words, R)
        xc_w = load_words("xc_w", xc_words, Q)
        xt_w = tile("xt_w", [P, T], U16)
        nc.sync.dma_start(xt_w[:].bitcast(I32), xt_words[0].bitcast(I32))
        idx2 = load_list("idx2", offs2)
        idx3 = load_list("idx3", offs3)
        w_raw = load_words("w_raw", w_words, R)
        wb_rows = tile("wb_rows", [4, QUADS, N // 4], I32)
        nc.sync.dma_start(wb_rows[:], by_quadrant(wb_scales))
        wb_w = tile("wb_w", [P, 2 * N], U8)
        nc.sync.dma_start(wb_w[:].bitcast(I32), wb_words[0].bitcast(I32))
        page_lists = [load_list("idx4", offs4), load_list("idx5", offs5)]

        def deal_words(name, src):
            dealt = tile(name, [P, PACK, P], U32)
            nc.scalar.copy(dealt[:].rearrange("p t (c i) -> p c t i", i=4), src.rearrange("p (c i t) -> p c t i", i=4, t=PACK))
            return dealt

        def deal_bytes(name, src, engine):
            dealt = tile(name, [P, PACK, P], U8)
            engine.tensor_copy(dealt[:], src.rearrange("p (m t) -> p t m", t=PACK))
            return dealt

        spread(planes, rows)
        wg_s = deal_bytes("wg_s", planes[:, 0:R], nc.vector)
        wg_w = deal_words("wg_w", wg_raw[:])
        g_ps = ps.tile([P, PACK, Q], F32, name="g_ps")
        for t in range(PACK):
            nc.tensor.matmul_mx(
                out=g_ps[:, t, :], lhsT=wg_w[:, t, :].bitcast(E5M2X4), lhsT_scale=wg_s[:, t, :],
                rhs=xc_w[:].bitcast(E4M3X4), rhs_scale=planes[:, 2 * R :], start=True, stop=True,
            )

        spread(xt_plane, xt_rows)
        xg_s = tile("xg_s", [P, J], U8)
        nc.vector.tensor_copy(xg_s[:], xt_plane[:].indirect(idx[:]))
        w_w = deal_words("w_w", w_raw[:])
        w_s = deal_bytes("w_s", planes[:, R : 2 * R], nc.vector)
        xg_w = tile("xg_w", [P, J], U16)
        nc.vector.tensor_copy(xg_w[:], xt_w[:].indirect(idx[:]))

        gains = tile("gains", [P, PACK, 2], F32)
        nc.scalar.copy(gains[:], g_ps[:, :, 0 : Q : O])
        g_bf = tile("g_bf", [P, Q, PACK], BF16, tag="w_raw")
        nc.scalar.copy(g_bf[:], g_ps[:].rearrange("p t q -> p q t"))

        a_ps = [ps.tile([P, J], F32, name="a_ps%d" % t) for t in range(PACK)]
        for t in range(PACK):
            nc.tensor.matmul_mx(
                out=a_ps[t][:], lhsT=w_w[:, t, :].bitcast(E4M3X4), lhsT_scale=w_s[:, t, :],
                rhs=xg_w[:].bitcast(E2M1X4), rhs_scale=xg_s[:], start=True, stop=True,
            )
        spread(wb_plane, wb_rows)

        def quantise(name, values):
            codes = tile(name + "_codes", [P, P], U32)
            plane = tile(name + "_plane", [P, P], U8)
            nc.vector.quantize_mx(out=codes[:].bitcast(E5M2X4), scales=plane[:], in_=values[:].rearrange("p d t -> p (d t)"))
            return codes, plane

        def project(bank, h, codes, plane):
            nc.tensor.matmul_mx(
                out=bank, lhsT=wb_w[:, 2 * P * h : 2 * P * (h + 1)].bitcast(E2M1X4), lhsT_scale=wb_plane[:, P * h : P * (h + 1)],
                rhs=codes[:].bitcast(E5M2X4), rhs_scale=plane[:], start=True, stop=True,
            )

        def put(engine, h, k, src, base, d0, d1):
            window = pages[h][k][:].indirect(page_lists[k][:, d0 // 16 : d1 // 16])
            if engine == "vector":
                nc.vector.tensor_copy(window, src[:, d0 - base : d1 - base])
            else:
                nc.scalar.activation(window, src[:, d0 - base : d1 - base], COPY)

        g_codes, g_plane = quantise("g", g_bf)

        h32 = tile("h32", [P, PACK, X], F32)
        for t in range(PACK):
            a_t = tile("a%d" % t, [P, J], F32)
            nc.vector.tensor_copy(a_t[:], a_ps[t][:])
            nc.scalar.activation(h32[:, t, 0:O], a_t[:].indirect(idx2[:]), COPY, scale=gains[:, t, 0:1])
            nc.scalar.activation(h32[:, t, O:X], a_t[:].indirect(idx3[:]), COPY, scale=gains[:, t, 1:2])

        pg_ps = ps.tile([P, 2, Q], F32, name="pg_ps")
        for h in range(2):
            project(pg_ps[:, h, :], h, g_codes, g_plane)
        pg = tile("pg", [P, 2, Q], F32)
        nc.vector.tensor_copy(pg[:], pg_ps[:])

        h_bf = tile("h_bf", [P, X, PACK], BF16)
        nc.vector.tensor_copy(h_bf[:].rearrange("p (c i) t -> p c t i", i=4), h32[:].rearrange("p t (c i) -> p c t i", i=4))
        h_codes, h_plane = quantise("h", h_bf)
        ph_ps = [ps.tile([P, X], F32, name="ph_ps%d" % h) for h in range(2)]
        for h in range(2):
            project(ph_ps[h][:], h, h_codes, h_plane)
        put("vector", 0, 0, pg[:, 0, :], X, X, D)
        put("scalar", 0, 1, pg[:, 0, :], X, X, D)
        put("scalar", 1, 1, pg[:, 1, :], X, X, D)
        put("scalar", 1, 0, pg[:, 1, :], X, X, D)
        ph = tile("ph", [P, 2, X], F32)
        nc.vector.tensor_copy(ph[:, 0, :], ph_ps[0][:])
        nc.scalar.copy(ph[:, 1, :], ph_ps[1][:])
        sums = [tile("sum%d" % h, [P, E], F32) for h in range(2)]
        for h in range(2):
            put("vector", h, 0, ph[:, h, :], 0, 0, X)
            put("scalar", h, 1, ph[:, h, :], 0, 0, X)
        nc.vector.tensor_tensor(sums[0][:], pages[0][0][:], pages[0][1][:], ADD)
        nc.sync.dma_start(out[0:P, :], sums[0][:])
        for c in range(2):
            cols = slice(c * E // 2, (c + 1) * E // 2)
            nc.vector.tensor_tensor(sums[1][:, cols], pages[1][0][:, cols], pages[1][1][:, cols], ADD)
            nc.sync.dma_start(out[P:N, cols], sums[1][:, cols])
